import numpy as np
import ml_dtypes


def mxq(x, axis, fmt="e4m3"):
    dtype, down = {"e4m3": (ml_dtypes.float8_e4m3fn, 7), "e5m2": (ml_dtypes.float8_e5m2, 14)}[fmt]
    v = np.moveaxis(np.asarray(x, np.float32).astype(ml_dtypes.bfloat16).astype(np.float64), axis, -1)
    blocks = v.reshape(v.shape[:-1] + (-1, 32))
    amax = np.abs(blocks).max(-1, keepdims=True)
    byte = np.maximum(np.where(amax > 0, np.frexp(amax)[1] - 1 + 127, 0) - down, 1)
    scale = np.exp2(byte - 127.0)
    codes = (blocks / scale).astype(np.float32).astype(dtype).astype(np.float64)
    return np.moveaxis((codes * scale).reshape(v.shape), -1, axis)


WIDE = False


def mx_kscale(k):
    if not WIDE:
        return np.ones(k)
    levels = np.array([10, -10, 5, -5, 0])
    if k % 512:
        return np.exp2(np.random.permutation(np.resize(levels, k // 32))).repeat(32)
    a = np.empty((k // 512, 16))
    for p in range(k // 512):
        a[p, :8] = np.random.permutation(np.resize(levels, 8))
        for g in range(8):
            far = levels[np.abs(levels - a[p, g]) >= 10]
            a[p, g + 8] = far[np.random.randint(len(far))]
    return np.exp2(a.ravel()).repeat(32)


def f64(x):
    return np.asarray(x).astype(np.float64)


def striped(idx):
    return np.tile(idx.reshape(-1, 16).T, (8, 1)).astype(np.uint16)


def unstriped(offs):
    return offs[:16].T.reshape(-1).astype(np.int64)


def pack_weight(w):
    k, n = w.shape
    w = f64(np.asarray(w, np.float32).astype(ml_dtypes.bfloat16)).reshape(k // 32, 32, n)
    amax = np.abs(w).max(1)
    byte = np.clip(np.where(amax > 0, np.frexp(amax)[1] - 1 + 127 - 7, 1), 1, 254)
    scaled = (w * np.exp2(127.0 - byte)[:, None, :]).reshape(k, n).astype(np.float32)
    words = np.ascontiguousarray(scaled.reshape(k // 512, 128, 4, n).transpose(0, 1, 3, 2)).astype(ml_dtypes.float8_e4m3fn).view(np.uint8)
    return words, np.ascontiguousarray(byte.astype(np.uint8).reshape(k // 512, 16, n))


def unpack_weight(words, scales):
    g, p, n, _ = words.shape
    vals = np.ascontiguousarray(words).view(ml_dtypes.float8_e4m3fn).astype(np.float64) * np.repeat(np.exp2(scales.astype(np.float64) - 127.0), 8, axis=1)[..., None]
    return vals.transpose(0, 1, 3, 2).reshape(g * 512, n)

def planes(y):
    n, m = y.shape
    v = y.astype(np.float32).astype(ml_dtypes.bfloat16).astype(np.float64).reshape(n // 32, 32, m)
    top = np.abs(v).max(1)
    byte = np.clip(np.where(top > 0, np.frexp(top)[1] - 1 + 127 - 7, 1), 1, 254)
    codes = (v * np.exp2(127.0 - byte)[:, None, :]).reshape(n, m).astype(np.float32).astype(ml_dtypes.float8_e4m3fn).view(np.uint8)
    words = codes.reshape(n // 512, 128, 4, m).transpose(0, 1, 3, 2)
    return np.ascontiguousarray(words), np.ascontiguousarray(byte.astype(np.uint8).reshape(n // 512, 16, m))


K, T, D, N = 512, 512, 4, 512
P = 2 ** 7


def setup_inputs():
    n = np.random.standard_normal
    s = mx_kscale(K)[:, None]
    packed_xT = pack_weight(n((K, T)) * s)
    return {
        "x_words": packed_xT[0],
        "x_scales": packed_xT[1],
        "w1": (n((K, N)) / np.sqrt(K) / s).astype(np.float32),
        "score": np.tile(np.random.standard_normal((D, 1, T)), (1, P, 1)).astype(np.float32),
        "pos1": striped(np.random.permutation(T)),
        "pos2": striped(np.random.permutation(T)),
        "pos3": striped(np.random.permutation(T)),
        "pos4": striped(np.random.permutation(T)),
    }


def reference(x_words, x_scales, w1, score, pos1, pos2, pos3, pos4):
    xq = unpack_weight(x_words, x_scales)
    y = mxq(f64(w1), 0, "e4m3").T @ xq
    e0 = np.exp(f64(score)[0, :1])
    e1 = np.exp(f64(score)[1, :1])
    e2 = np.exp(f64(score)[2, :1])
    e3 = np.exp(f64(score)[3, :1])
    num = y[:, unstriped(pos1)] * e0 + y[:, unstriped(pos2)] * e1 + y[:, unstriped(pos3)] * e2 + y[:, unstriped(pos4)] * e3
    den = e0 + e1 + e2 + e3
    out_0 = num / den
    return (out_0,) + planes(out_0)

@@ -1,0 +1,195 @@
+from contextlib import ExitStack
+
+import concourse.mybir as mybir
+from concourse.masks import make_identity
+
+K, T, D, N = 512, 512, 4, 512
+P = 128
+PACK = 4
+BLOCKS = N // P
+FLOPS = 2 * K * N * T
+BYTES = K * T + K * T // 32 + 4 * K * N + 4 * D * T + 2 * D * P * T // 16 + 4 * N * T + N * T + N * T // 32
+
+F32 = mybir.dt.float32
+BF16 = mybir.dt.bfloat16
+U32 = mybir.dt.uint32
+I32 = mybir.dt.int32
+U16 = mybir.dt.uint16
+U8 = mybir.dt.uint8
+FP8X4 = mybir.dt.float8_e4m3fn_x4
+ALU = mybir.AluOpType
+ACT = mybir.ActivationFunctionType
+AXIS_X = mybir.AxisListType.X
+
+CHUNKS = ((0, 256), (256, 128), (384, 128))
+
+
+def tile_picked_wgatv_none_lo_kernel(
+    tc, x_words, x_scales, w1, score, pos1, pos2, pos3, pos4, out_0, out_1, out_2
+):
+    nc = tc.nc
+    with ExitStack() as ctx:
+        keep = ctx.enter_context(tc.tile_pool(name="keep", bufs=1))
+        ring = ctx.enter_context(tc.tile_pool(name="ring", bufs=8))
+        banks = ctx.enter_context(tc.psum_pool(name="banks", bufs=4))
+
+        x_scale = keep.tile([P, T], U8, name="x_scale", align_bytes=64)
+        nc.vector.memset(x_scale[:].bitcast(I32), 0)
+        score_rows = keep.tile([P, P], F32, name="score_rows")
+        nc.vector.memset(score_rows[:], 0.0)
+        ident = keep.tile([P, P], F32, name="ident")
+        make_identity(nc, ident[:])
+        warm = keep.tile([P, 1], F32, name="warm")
+        nc.scalar.activation(warm[:], score_rows[:, 0:1], ACT.Exp)
+
+        w_view = w1.rearrange("(p j) m -> p j m", j=PACK)
+        w_raw0 = keep.tile([P, PACK, P], F32, name="w_raw0", tag="w_stage")
+        nc.sync.dma_start(w_raw0[:], w_view[:, :, 0:P])
+        x_code = keep.tile([P, T], U32, name="x_code", align_bytes=64)
+        nc.sync.dma_start(x_code[:].bitcast(I32), x_words[0].rearrange("p c r -> p (c r)").bitcast(I32))
+        score_view = score.rearrange("d r (b n) -> (d r b) n", n=P)
+        nc.sync.dma_start(score_rows[0 : D * BLOCKS, :], score_view[0 : D * P * BLOCKS : P + 1, :])
+        for q in range(4):
+            nc.sync.dma_start(x_scale[32 * q : 32 * q + 4, :].bitcast(I32), x_scales[0, 4 * q : 4 * q + 4, :].bitcast(I32))
+        lists = []
+        for d, pos in enumerate((pos1, pos2, pos3, pos4)):
+            offsets = keep.tile([P, T // 16], U16, name="offsets%d" % d)
+            nc.sync.dma_start(offsets[:], pos)
+            lists.append(offsets)
+        w_raw = [w_raw0[:]]
+
+        y = []
+
+        def project(b):
+            grouped = keep.tile([P, P, PACK], BF16, name="w_grouped%d" % b, align_bytes=64)
+            if b < 1:
+                nc.vector.tensor_copy(grouped[:], w_raw[b].rearrange("p j m -> p m j"))
+            else:
+                nc.scalar.copy(grouped[:], w_raw[b].rearrange("p j m -> p m j"))
+            w_code = keep.tile([P, P], U32, name="w_code%d" % b, align_bytes=64)
+            w_scale = keep.tile([P, P], U8, name="w_scale%d" % b, align_bytes=64)
+            nc.vector.quantize_mx(
+                out=w_code[:].bitcast(FP8X4), scales=w_scale[:], in_=grouped[:].rearrange("p m j -> p (m j)")
+            )
+            bank = banks.tile([P, T], F32, name="io")
+            nc.tensor.matmul_mx(
+                out=bank[:],
+                lhsT=w_code[:].bitcast(FP8X4),
+                lhsT_scale=w_scale[:],
+                rhs=x_code[:].bitcast(FP8X4),
+                rhs_scale=x_scale[:],
+                start=True,
+                stop=True,
+            )
+            rows = keep.tile([P, T], F32, name="y%d" % b)
+            nc.scalar.copy(rows[:], bank[:])
+            y.append(rows)
+
+        turned = banks.tile([P, T], F32, name="io")
+        nc.tensor.transpose(turned[:, 0:P], score_rows[:], ident[:])
+        scores = turned[:, 0 : D * BLOCKS].rearrange("p (d b) -> p d b", d=D)
+        top = keep.tile([P, BLOCKS], F32, name="top")
+        nc.vector.tensor_reduce(top[:], scores.rearrange("p d b -> p b d"), AXIS_X, ALU.max)
+        shifted = keep.tile([P, D, BLOCKS], F32, name="shifted")
+        nc.vector.tensor_tensor(shifted[:], scores, top[:].unsqueeze(1).to_broadcast([P, D, BLOCKS]), ALU.subtract)
+
+        def spread(c):
+            v0, width = CHUNKS[c]
+            weights = keep.tile([P, D, width], F32, name="weights%d" % c)
+            per_bank = T // width
+            for d0 in range(0, D, per_bank):
+                bank = banks.tile([P, T], F32, name="io")
+                for d in range(d0, d0 + per_bank):
+                    for j in range(width // P):
+                        col = (d - d0) * width + j * P
+                        nc.tensor.transpose(
+                            bank[:, col : col + P],
+                            shifted[:, d, v0 // P + j : v0 // P + j + 1].to_broadcast([P, P]),
+                            ident[:],
+                        )
+                nc.scalar.activation(
+                    weights[:, d0 : d0 + per_bank, :].rearrange("p d v -> p (d v)"), bank[:], ACT.Exp
+                )
+            return weights
+
+        project(0)
+        w_rest = keep.tile([P, PACK, N - P], F32, name="w_rest", tag="w_stage")
+        nc.sync.dma_start(w_rest[:, :, 0:P], w_view[:, :, P : 2 * P])
+        nc.sync.dma_start(w_rest[:, :, P:], w_view[:, :, 2 * P :])
+        w_raw.extend(w_rest[:, :, b * P : (b + 1) * P] for b in range(BLOCKS - 1))
+        weights = [spread(0)]
+        project(1)
+        exps = keep.tile([P, D, BLOCKS], F32, name="exps")
+        nc.scalar.activation(exps[:], shifted[:], ACT.Exp)
+        total = keep.tile([P, BLOCKS], F32, name="total")
+        nc.vector.tensor_reduce(total[:], exps[:].rearrange("p d b -> p b d"), AXIS_X, ALU.add)
+        inverse = keep.tile([P, BLOCKS], F32, name="inverse")
+        nc.vector.reciprocal(inverse[:], total[:])
+        project(2)
+        project(3)
+        weights.append(spread(1))
+        weights.append(spread(2))
+
+        out_code = keep.tile([P, T], U32, name="out_code", align_bytes=64)
+        out_scale = keep.tile([P, T], U8, name="out_scale", align_bytes=64)
+        out_view = out_0.rearrange("(q t) v -> q t v", t=PACK)
+        code_view = out_1[0].rearrange("q v t -> q (v t)").bitcast(I32)
+
+        for c, (v0, width) in enumerate(CHUNKS):
+            last = c == len(CHUNKS) - 1
+            groups = width // P
+            sums = [banks.tile([P, N], F32, name="sums") for j in range(groups)]
+            dealt = [keep.tile([P, PACK, P], F32, name="dealt%d_%d" % (c, j)) for j in range(groups)]
+
+            def drain(j, bank, b0, b1):
+                nc.scalar.activation(
+                    dealt[j][:, :, 32 * b0 : 32 * b1],
+                    bank[:, b0 * P : b1 * P].rearrange("v (q t) -> v t q", t=PACK),
+                    ACT.Copy,
+                    scale=inverse[:, v0 // P + j : v0 // P + j + 1],
+                )
+
+            for b in range(BLOCKS):
+                if last and b == BLOCKS - 1:
+                    drain(0, sums[0], 0, b)
+                    sums = [banks.tile([P, N], F32, name="sums")]
+                for d in range(D):
+                    picked = ring.tile([P, width], F32, name="picked")
+                    nc.vector.tensor_tensor(
+                        picked[:],
+                        y[b][:].indirect(lists[d][:, v0 // 16 : (v0 + width) // 16]),
+                        weights[c][:, d, :],
+                        ALU.mult,
+                    )
+                    for j in range(groups):
+                        nc.tensor.matmul(
+                            sums[j][:, b * P : (b + 1) * P],
+                            picked[:, j * P : (j + 1) * P],
+                            ident[:],
+                            start=(d == 0),
+                            stop=(d == D - 1),
+                            is_transpose=True,
+                        )
+            result = keep.tile([P, PACK, width], F32, name="result%d" % c)
+            rounded = keep.tile([P, width, PACK], BF16, name="rounded%d" % c, align_bytes=64)
+            for j in range(groups):
+                drain(j, sums[j], BLOCKS - 1 if last else 0, BLOCKS)
+                back = banks.tile([P, PACK, P], F32, name="io")
+                for t in range(PACK):
+                    nc.tensor.transpose(back[:, t, :], dealt[j][:, t, :], ident[:])
+                if last:
+                    nc.vector.tensor_copy(rounded[:], back[:].rearrange("q t v -> q v t"))
+                    nc.scalar.copy(result[:], back[:])
+                else:
+                    nc.scalar.copy(result[:, :, j * P : (j + 1) * P], back[:])
+                    nc.scalar.copy(rounded[:, j * P : (j + 1) * P, :], back[:].rearrange("q t v -> q v t"))
+            nc.vector.quantize_mx(
+                out=out_code[:, v0 : v0 + width].bitcast(FP8X4),
+                scales=out_scale[:, v0 : v0 + width],
+                in_=rounded[:].rearrange("q v t -> q (v t)"),
+            )
+            nc.sync.dma_start(out_view[:, :, v0 : v0 + width], result[:])
+            nc.sync.dma_start(code_view[:, v0 : v0 + width], out_code[:, v0 : v0 + width].bitcast(I32))
+        for q in range(4):
+            queue = nc.sync if q % 2 else nc.scalar
+            queue.dma_start(out_2[0, 4 * q : 4 * q + 4, :].bitcast(I32), out_scale[32 * q : 32 * q + 4, :].bitcast(I32))

@@ -21,6 +21,7 @@ ALU = mybir.AluOpType
 ACT = mybir.ActivationFunctionType
 AXIS_X = mybir.AxisListType.X
 
+SPARE = P - D * BLOCKS
 CHUNKS = ((0, 256), (256, 128), (384, 128))
 
 
@@ -31,38 +32,45 @@ def tile_picked_wgatv_none_lo_kernel(
     with ExitStack() as ctx:
         keep = ctx.enter_context(tc.tile_pool(name="keep", bufs=1))
         ring = ctx.enter_context(tc.tile_pool(name="ring", bufs=8))
-        banks = ctx.enter_context(tc.psum_pool(name="banks", bufs=4))
+        banks = ctx.enter_context(tc.psum_pool(name="banks", bufs=1))
+
+        bank_tiles = [banks.tile([P, T], F32, name="bank%d" % i) for i in range(7)]
+
+        def bank_tile(index, width):
+            return bank_tiles[index][:, 0:width]
 
         x_scale = keep.tile([P, T], U8, name="x_scale", align_bytes=64)
         nc.vector.memset(x_scale[:].bitcast(I32), 0)
         score_rows = keep.tile([P, P], F32, name="score_rows")
-        nc.vector.memset(score_rows[:], 0.0)
+        nc.vector.memset(score_rows[0:SPARE, :], 0.0)
         ident = keep.tile([P, P], F32, name="ident")
         make_identity(nc, ident[:])
-        warm = keep.tile([P, 1], F32, name="warm")
-        nc.scalar.activation(warm[:], score_rows[:, 0:1], ACT.Exp)
 
+        score_view = score.rearrange("d r (b n) -> (d r b) n", n=P)
+        nc.sync.dma_start(score_rows[SPARE:P, :], score_view[0 : D * P * BLOCKS : P + 1, :])
         w_view = w1.rearrange("(p j) m -> p j m", j=PACK)
-        w_raw0 = keep.tile([P, PACK, P], F32, name="w_raw0", tag="w_stage")
+        w_stage = keep.tile([P, PACK, 2 * P], F32, name="w_stage")
+        w_raw0 = w_stage[:].rearrange("p j m -> p (j m)")[:, 0 : PACK * P].rearrange("p (j m) -> p j m", j=PACK)
         nc.sync.dma_start(w_raw0[:], w_view[:, :, 0:P])
         x_code = keep.tile([P, T], U32, name="x_code", align_bytes=64)
         nc.sync.dma_start(x_code[:].bitcast(I32), x_words[0].rearrange("p c r -> p (c r)").bitcast(I32))
-        score_view = score.rearrange("d r (b n) -> (d r b) n", n=P)
-        nc.sync.dma_start(score_rows[0 : D * BLOCKS, :], score_view[0 : D * P * BLOCKS : P + 1, :])
         for q in range(4):
             nc.sync.dma_start(x_scale[32 * q : 32 * q + 4, :].bitcast(I32), x_scales[0, 4 * q : 4 * q + 4, :].bitcast(I32))
+        w_raw1 = keep.tile([P, PACK, P], F32, name="w_raw1")
+        nc.sync.dma_start(w_raw1[:], w_view[:, :, P : 2 * P])
         lists = []
         for d, pos in enumerate((pos1, pos2, pos3, pos4)):
             offsets = keep.tile([P, T // 16], U16, name="offsets%d" % d)
             nc.sync.dma_start(offsets[:], pos)
             lists.append(offsets)
-        w_raw = [w_raw0[:]]
+        w_raw = [w_raw0[:], w_raw1[:], w_stage[:, :, 0:P], w_stage[:, :, P : 2 * P]]
 
         y = []
+        w_grouped = [keep.tile([P, P, PACK], BF16, name="w_grouped%d" % b, align_bytes=64) for b in range(BLOCKS - 1)]
 
         def project(b):
-            grouped = keep.tile([P, P, PACK], BF16, name="w_grouped%d" % b, align_bytes=64)
-            if b < 1:
+            grouped = w_grouped[max(b - 1, 0)]
+            if b < 2:
                 nc.vector.tensor_copy(grouped[:], w_raw[b].rearrange("p j m -> p m j"))
             else:
                 nc.scalar.copy(grouped[:], w_raw[b].rearrange("p j m -> p m j"))
@@ -71,64 +79,68 @@ def tile_picked_wgatv_none_lo_kernel(
             nc.vector.quantize_mx(
                 out=w_code[:].bitcast(FP8X4), scales=w_scale[:], in_=grouped[:].rearrange("p m j -> p (m j)")
             )
-            bank = banks.tile([P, T], F32, name="io")
-            nc.tensor.matmul_mx(
-                out=bank[:],
-                lhsT=w_code[:].bitcast(FP8X4),
-                lhsT_scale=w_scale[:],
-                rhs=x_code[:].bitcast(FP8X4),
-                rhs_scale=x_scale[:],
-                start=True,
-                stop=True,
-            )
             rows = keep.tile([P, T], F32, name="y%d" % b)
-            nc.scalar.copy(rows[:], bank[:])
+            parts = 2 if b == 0 else 1
+            for h in range(parts):
+                cols = slice(h * T // parts, (h + 1) * T // parts)
+                bank = bank_tile((h, 2, 1, 2)[b], T // parts)
+                nc.tensor.matmul_mx(
+                    out=bank[:],
+                    lhsT=w_code[:].bitcast(FP8X4),
+                    lhsT_scale=w_scale[:],
+                    rhs=x_code[:, cols].bitcast(FP8X4),
+                    rhs_scale=x_scale[:, cols],
+                    start=True,
+                    stop=True,
+                )
+                if h == 1:
+                    nc.vector.tensor_copy(rows[:, cols], bank[:])
+                else:
+                    nc.scalar.copy(rows[:, cols], bank[:])
             y.append(rows)
 
-        turned = banks.tile([P, T], F32, name="io")
+        turned = bank_tile(0, P)
         nc.tensor.transpose(turned[:, 0:P], score_rows[:], ident[:])
-        scores = turned[:, 0 : D * BLOCKS].rearrange("p (d b) -> p d b", d=D)
-        top = keep.tile([P, BLOCKS], F32, name="top")
+        scores = turned[:, SPARE:P].rearrange("p (d b) -> p d b", d=D)
+        top = w_grouped[0][:].rearrange("p m j -> p (m j)").bitcast(F32)[:, 0:BLOCKS]
         nc.vector.tensor_reduce(top[:], scores.rearrange("p d b -> p b d"), AXIS_X, ALU.max)
         shifted = keep.tile([P, D, BLOCKS], F32, name="shifted")
         nc.vector.tensor_tensor(shifted[:], scores, top[:].unsqueeze(1).to_broadcast([P, D, BLOCKS]), ALU.subtract)
 
-        def spread(c):
-            v0, width = CHUNKS[c]
-            weights = keep.tile([P, D, width], F32, name="weights%d" % c)
-            per_bank = T // width
-            for d0 in range(0, D, per_bank):
-                bank = banks.tile([P, T], F32, name="io")
-                for d in range(d0, d0 + per_bank):
-                    for j in range(width // P):
-                        col = (d - d0) * width + j * P
-                        nc.tensor.transpose(
-                            bank[:, col : col + P],
-                            shifted[:, d, v0 // P + j : v0 // P + j + 1].to_broadcast([P, P]),
-                            ident[:],
-                        )
-                nc.scalar.activation(
-                    weights[:, d0 : d0 + per_bank, :].rearrange("p d v -> p (d v)"), bank[:], ACT.Exp
-                )
-            return weights
-
-        project(0)
-        w_rest = keep.tile([P, PACK, N - P], F32, name="w_rest", tag="w_stage")
-        nc.sync.dma_start(w_rest[:, :, 0:P], w_view[:, :, P : 2 * P])
-        nc.sync.dma_start(w_rest[:, :, P:], w_view[:, :, 2 * P :])
-        w_raw.extend(w_rest[:, :, b * P : (b + 1) * P] for b in range(BLOCKS - 1))
-        weights = [spread(0)]
-        project(1)
         exps = keep.tile([P, D, BLOCKS], F32, name="exps")
         nc.scalar.activation(exps[:], shifted[:], ACT.Exp)
+
+        weights = [
+            keep.tile([P, D, width], F32, name="weights%d" % c) for c, (v0, width) in enumerate(CHUNKS)
+        ]
+
+        def spread(c, d0, d1, index):
+            v0, width = CHUNKS[c]
+            bank = bank_tile(index, (d1 - d0) * width)
+            for d in range(d0, d1):
+                for j in range(width // P):
+                    col = (d - d0) * width + j * P
+                    nc.tensor.transpose(
+                        bank[:, col : col + P],
+                        shifted[:, d, v0 // P + j : v0 // P + j + 1].to_broadcast([P, P]),
+                        ident[:],
+                    )
+            nc.scalar.activation(weights[c][:, d0:d1, :].rearrange("p d v -> p (d v)"), bank[:], ACT.Exp)
+
+        spread(0, 0, 1, 1)
+        spread(0, 1, 2, 2)
+        project(0)
+        nc.sync.dma_start(w_stage[:], w_view[:, :, 2 * P : 4 * P])
+        spread(0, 2, 4, 0)
+        project(1)
         total = keep.tile([P, BLOCKS], F32, name="total")
         nc.vector.tensor_reduce(total[:], exps[:].rearrange("p d b -> p b d"), AXIS_X, ALU.add)
         inverse = keep.tile([P, BLOCKS], F32, name="inverse")
         nc.vector.reciprocal(inverse[:], total[:])
         project(2)
         project(3)
-        weights.append(spread(1))
-        weights.append(spread(2))
+        spread(1, 0, D, 1)
+        spread(2, 0, D, 2)
 
         out_code = keep.tile([P, T], U32, name="out_code", align_bytes=64)
         out_scale = keep.tile([P, T], U8, name="out_scale", align_bytes=64)
@@ -138,7 +150,7 @@ def tile_picked_wgatv_none_lo_kernel(
         for c, (v0, width) in enumerate(CHUNKS):
             last = c == len(CHUNKS) - 1
             groups = width // P
-            sums = [banks.tile([P, N], F32, name="sums") for j in range(groups)]
+            sums = [bank_tile((5, 6, 0, 3)[v0 // P + j], N) for j in range(groups)]
             dealt = [keep.tile([P, PACK, P], F32, name="dealt%d_%d" % (c, j)) for j in range(groups)]
 
             def drain(j, bank, b0, b1):
@@ -152,7 +164,7 @@ def tile_picked_wgatv_none_lo_kernel(
             for b in range(BLOCKS):
                 if last and b == BLOCKS - 1:
                     drain(0, sums[0], 0, b)
-                    sums = [banks.tile([P, N], F32, name="sums")]
+                    sums = [bank_tile(4, N)]
                 for d in range(D):
                     picked = ring.tile([P, width], F32, name="picked")
                     nc.vector.tensor_tensor(
@@ -174,12 +186,16 @@ def tile_picked_wgatv_none_lo_kernel(
             rounded = keep.tile([P, width, PACK], BF16, name="rounded%d" % c, align_bytes=64)
             for j in range(groups):
                 drain(j, sums[j], BLOCKS - 1 if last else 0, BLOCKS)
-                back = banks.tile([P, PACK, P], F32, name="io")
+                back = bank_tile(1 + (v0 // P + j) % 2, N).rearrange("q (t v) -> q t v", t=PACK)
                 for t in range(PACK):
                     nc.tensor.transpose(back[:, t, :], dealt[j][:, t, :], ident[:])
                 if last:
                     nc.vector.tensor_copy(rounded[:], back[:].rearrange("q t v -> q v t"))
-                    nc.scalar.copy(result[:], back[:])
+                    for h in range(2):
+                        rows = slice(2 * h, 2 * h + 2)
+                        nc.scalar.copy(result[:, rows, :], back[:, rows, :])
+                        queue = nc.scalar if h else nc.sync
+                        queue.dma_start(out_view[:, rows, v0 : v0 + width], result[:, rows, :])
                 else:
                     nc.scalar.copy(result[:, :, j * P : (j + 1) * P], back[:])
                     nc.scalar.copy(rounded[:, j * P : (j + 1) * P, :], back[:].rearrange("q t v -> q v t"))
@@ -188,8 +204,9 @@ def tile_picked_wgatv_none_lo_kernel(
                 scales=out_scale[:, v0 : v0 + width],
                 in_=rounded[:].rearrange("q v t -> q (v t)"),
             )
-            nc.sync.dma_start(out_view[:, :, v0 : v0 + width], result[:])
+            if not last:
+                nc.sync.dma_start(out_view[:, :, v0 : v0 + width], result[:])
             nc.sync.dma_start(code_view[:, v0 : v0 + width], out_code[:, v0 : v0 + width].bitcast(I32))
         for q in range(4):
-            queue = nc.sync if q % 2 else nc.scalar
+            queue = nc.sync if q < 2 else nc.scalar
             queue.dma_start(out_2[0, 4 * q : 4 * q + 4, :].bitcast(I32), out_scale[32 * q : 32 * q + 4, :].bitcast(I32))

@@ -6,7 +6,11 @@ from concourse.masks import make_identity
 K, T, D, N = 512, 512, 4, 512
 P = 128
 PACK = 4
+QUAD = 32
 BLOCKS = N // P
+GROUPS = T // P
+SPARE = P - D * GROUPS
+PAD = 8
 FLOPS = 2 * K * N * T
 BYTES = K * T + K * T // 32 + 4 * K * N + 4 * D * T + 2 * D * P * T // 16 + 4 * N * T + N * T + N * T // 32
 
@@ -21,7 +25,6 @@ ALU = mybir.AluOpType
 ACT = mybir.ActivationFunctionType
 AXIS_X = mybir.AxisListType.X
 
-SPARE = P - D * BLOCKS
 CHUNKS = ((0, 256), (256, 128), (384, 128))
 
 
@@ -31,61 +34,61 @@ def tile_picked_wgatv_none_lo_kernel(
     nc = tc.nc
     with ExitStack() as ctx:
         keep = ctx.enter_context(tc.tile_pool(name="keep", bufs=1))
-        ring = ctx.enter_context(tc.tile_pool(name="ring", bufs=8))
-        banks = ctx.enter_context(tc.psum_pool(name="banks", bufs=1))
-
-        bank_tiles = [banks.tile([P, T], F32, name="bank%d" % i) for i in range(7)]
-
-        def bank_tile(index, width):
-            return bank_tiles[index][:, 0:width]
+        ring = ctx.enter_context(tc.tile_pool(name="ring", bufs=12))
+        psum = ctx.enter_context(tc.psum_pool(name="psum", bufs=1))
+        work = [psum.tile([P, T], F32, name="work%d" % i) for i in range(3)]
+        sums = [psum.tile([P, N], F32, name="sums%d" % g) for g in range(GROUPS)]
 
         x_scale = keep.tile([P, T], U8, name="x_scale", align_bytes=64)
         nc.vector.memset(x_scale[:].bitcast(I32), 0)
-        score_rows = keep.tile([P, P], F32, name="score_rows")
+        staged = keep.tile([P, P * PACK], BF16, name="staged", align_bytes=64)
+        score_rows = staged[:].bitcast(F32)[:, 0:P]
         nc.vector.memset(score_rows[0:SPARE, :], 0.0)
+        y = [keep.tile([P, T + PAD if b == 0 else T], F32, name="y%d" % b) for b in range(BLOCKS)]
+        nc.vector.memset(y[0][:, T:], 0.0)
         ident = keep.tile([P, P], F32, name="ident")
         make_identity(nc, ident[:])
 
-        score_view = score.rearrange("d r (b n) -> (d r b) n", n=P)
-        nc.sync.dma_start(score_rows[SPARE:P, :], score_view[0 : D * P * BLOCKS : P + 1, :])
+        score_view = score.rearrange("d r (g n) -> (d r g) n", n=P)
+        nc.sync.dma_start(score_rows[SPARE:P, :], score_view[0 : D * P * GROUPS : P + 1, :])
         w_view = w1.rearrange("(p j) m -> p j m", j=PACK)
-        w_stage = keep.tile([P, PACK, 2 * P], F32, name="w_stage")
-        w_raw0 = w_stage[:].rearrange("p j m -> p (j m)")[:, 0 : PACK * P].rearrange("p (j m) -> p j m", j=PACK)
-        nc.sync.dma_start(w_raw0[:], w_view[:, :, 0:P])
+        w_first = keep.tile([P, PACK, P], F32, name="w_first")
+        nc.sync.dma_start(w_first[:], w_view[:, :, 0:P])
         x_code = keep.tile([P, T], U32, name="x_code", align_bytes=64)
         nc.sync.dma_start(x_code[:].bitcast(I32), x_words[0].rearrange("p c r -> p (c r)").bitcast(I32))
-        for q in range(4):
-            nc.sync.dma_start(x_scale[32 * q : 32 * q + 4, :].bitcast(I32), x_scales[0, 4 * q : 4 * q + 4, :].bitcast(I32))
-        w_raw1 = keep.tile([P, PACK, P], F32, name="w_raw1")
-        nc.sync.dma_start(w_raw1[:], w_view[:, :, P : 2 * P])
-        lists = []
-        for d, pos in enumerate((pos1, pos2, pos3, pos4)):
-            offsets = keep.tile([P, T // 16], U16, name="offsets%d" % d)
+        w_second = keep.tile([P, PACK, P], F32, name="w_second")
+        nc.sync.dma_start(w_second[:], w_view[:, :, P : 2 * P])
+        for q in range(P // QUAD):
+            nc.sync.dma_start(
+                x_scale[QUAD * q : QUAD * q + 4, :].bitcast(I32), x_scales[0, 4 * q : 4 * q + 4, :].bitcast(I32)
+            )
+        lists = [keep.tile([P, T // 16], U16, name="offsets%d" % d) for d in range(D)]
+        nc.sync.dma_start(lists[0][:], pos1)
+        w_rest = keep.tile([P, PACK, 2 * P], F32, name="w_rest")
+        nc.sync.dma_start(w_rest[:], w_view[:, :, 2 * P : 4 * P])
+        for offsets, pos in zip(lists[1:], (pos2, pos3, pos4)):
             nc.sync.dma_start(offsets[:], pos)
-            lists.append(offsets)
-        w_raw = [w_raw0[:], w_raw1[:], w_stage[:, :, 0:P], w_stage[:, :, P : 2 * P]]
+        w_raw = [w_first[:], w_second[:], w_rest[:, :, 0:P], w_rest[:, :, P : 2 * P]]
 
-        y = []
-        w_grouped = [keep.tile([P, P, PACK], BF16, name="w_grouped%d" % b, align_bytes=64) for b in range(BLOCKS - 1)]
+        first = keep.tile([P, T], F32, name="first", align_bytes=64)
 
-        def project(b):
-            grouped = w_grouped[max(b - 1, 0)]
+        def project(b, banks):
             if b < 2:
-                nc.vector.tensor_copy(grouped[:], w_raw[b].rearrange("p j m -> p m j"))
+                grouped = staged[:]
+                nc.vector.tensor_copy(
+                    grouped.rearrange("p (m j) -> p m j", j=PACK), w_raw[b].rearrange("p j m -> p m j")
+                )
             else:
-                nc.scalar.copy(grouped[:], w_raw[b].rearrange("p j m -> p m j"))
+                grouped = first[:, T // 2 :].bitcast(BF16)
+                nc.scalar.copy(grouped.rearrange("p (m j) -> p m j", j=PACK), w_raw[b].rearrange("p j m -> p m j"))
             w_code = keep.tile([P, P], U32, name="w_code%d" % b, align_bytes=64)
             w_scale = keep.tile([P, P], U8, name="w_scale%d" % b, align_bytes=64)
-            nc.vector.quantize_mx(
-                out=w_code[:].bitcast(FP8X4), scales=w_scale[:], in_=grouped[:].rearrange("p m j -> p (m j)")
-            )
-            rows = keep.tile([P, T], F32, name="y%d" % b)
-            parts = 2 if b == 0 else 1
-            for h in range(parts):
-                cols = slice(h * T // parts, (h + 1) * T // parts)
-                bank = bank_tile((h, 2, 1, 2)[b], T // parts)
+            nc.vector.quantize_mx(out=w_code[:].bitcast(FP8X4), scales=w_scale[:], in_=grouped)
+            width = T // len(banks)
+            for h, bank in enumerate(banks):
+                cols = slice(h * width, (h + 1) * width)
                 nc.tensor.matmul_mx(
-                    out=bank[:],
+                    out=bank[:, 0:width],
                     lhsT=w_code[:].bitcast(FP8X4),
                     lhsT_scale=w_scale[:],
                     rhs=x_code[:, cols].bitcast(FP8X4),
@@ -93,112 +96,103 @@ def tile_picked_wgatv_none_lo_kernel(
                     start=True,
                     stop=True,
                 )
-                if h == 1:
-                    nc.vector.tensor_copy(rows[:, cols], bank[:])
+                if h == len(banks) - 1:
+                    nc.scalar.copy(y[b][:, cols], bank[:, 0:width])
                 else:
-                    nc.scalar.copy(rows[:, cols], bank[:])
-            y.append(rows)
+                    nc.vector.tensor_copy(y[b][:, cols], bank[:, 0:width])
 
-        turned = bank_tile(0, P)
-        nc.tensor.transpose(turned[:, 0:P], score_rows[:], ident[:])
-        scores = turned[:, SPARE:P].rearrange("p (d b) -> p d b", d=D)
-        top = w_grouped[0][:].rearrange("p m j -> p (m j)").bitcast(F32)[:, 0:BLOCKS]
-        nc.vector.tensor_reduce(top[:], scores.rearrange("p d b -> p b d"), AXIS_X, ALU.max)
-        shifted = keep.tile([P, D, BLOCKS], F32, name="shifted")
-        nc.vector.tensor_tensor(shifted[:], scores, top[:].unsqueeze(1).to_broadcast([P, D, BLOCKS]), ALU.subtract)
+        nc.tensor.transpose(work[0][:, 0:P], score_rows, ident[:])
+        scores = work[0][:, SPARE:P].rearrange("p (d g) -> p d g", d=D)
+        top = keep.tile([P, GROUPS], F32, name="top")
+        nc.vector.tensor_reduce(top[:], scores.rearrange("p d g -> p g d"), AXIS_X, ALU.max)
+        shifted = keep.tile([P, D, GROUPS], F32, name="shifted")
+        nc.vector.tensor_tensor(shifted[:], scores, top[:].unsqueeze(1).to_broadcast([P, D, GROUPS]), ALU.subtract)
 
-        exps = keep.tile([P, D, BLOCKS], F32, name="exps")
-        nc.scalar.activation(exps[:], shifted[:], ACT.Exp)
+        weights = [keep.tile([P, T], F32, name="weights%d" % d) for d in range(D)]
 
-        weights = [
-            keep.tile([P, D, width], F32, name="weights%d" % c) for c, (v0, width) in enumerate(CHUNKS)
-        ]
+        def spread(d, bank):
+            for g in range(GROUPS):
+                nc.tensor.transpose(
+                    bank[:, g * P : (g + 1) * P], shifted[:, d, g : g + 1].to_broadcast([P, P]), ident[:]
+                )
+            nc.scalar.activation(weights[d][:], bank[:], ACT.Exp)
 
-        def spread(c, d0, d1, index):
-            v0, width = CHUNKS[c]
-            bank = bank_tile(index, (d1 - d0) * width)
-            for d in range(d0, d1):
-                for j in range(width // P):
-                    col = (d - d0) * width + j * P
-                    nc.tensor.transpose(
-                        bank[:, col : col + P],
-                        shifted[:, d, v0 // P + j : v0 // P + j + 1].to_broadcast([P, P]),
-                        ident[:],
-                    )
-            nc.scalar.activation(weights[c][:, d0:d1, :].rearrange("p d v -> p (d v)"), bank[:], ACT.Exp)
+        def gather(b, d, v0, width, picked, targets):
+            nc.vector.tensor_tensor(
+                picked[:],
+                y[b][:].indirect(lists[d][:, v0 // 16 : (v0 + width) // 16]),
+                weights[d][:, v0 : v0 + width],
+                ALU.mult,
+            )
+            for j, bank in enumerate(targets):
+                nc.tensor.matmul(
+                    bank[:, b * P : (b + 1) * P],
+                    picked[:, j * P : (j + 1) * P],
+                    ident[:],
+                    start=(d == 0),
+                    stop=(d == D - 1),
+                    is_transpose=True,
+                )
 
-        spread(0, 0, 1, 1)
-        spread(0, 1, 2, 2)
-        project(0)
-        nc.sync.dma_start(w_stage[:], w_view[:, :, 2 * P : 4 * P])
-        spread(0, 2, 4, 0)
-        project(1)
-        total = keep.tile([P, BLOCKS], F32, name="total")
-        nc.vector.tensor_reduce(total[:], exps[:].rearrange("p d b -> p b d"), AXIS_X, ALU.add)
-        inverse = keep.tile([P, BLOCKS], F32, name="inverse")
+        spread(0, work[1])
+        project(0, [work[0], work[2]])
+        spread(1, work[0])
+        spread(2, work[2])
+        project(1, [work[1]])
+        spread(3, work[0])
+
+        gather(0, 0, 0, T, first, sums)
+        project(2, [work[1]])
+        project(3, [work[2]])
+        exps = first[:, 0 : D * GROUPS].rearrange("p (d g) -> p d g", d=D)
+        nc.scalar.activation(exps, shifted[:], ACT.Exp)
+        total = keep.tile([P, GROUPS], F32, name="total")
+        nc.vector.tensor_reduce(total[:], exps.rearrange("p d g -> p g d"), AXIS_X, ALU.add)
+        inverse = keep.tile([P, GROUPS], F32, name="inverse")
         nc.vector.reciprocal(inverse[:], total[:])
-        project(2)
-        project(3)
-        spread(1, 0, D, 1)
-        spread(2, 0, D, 2)
+        for d in range(1, D):
+            gather(0, d, 0, T, ring.tile([P, T], F32, name="picked"), sums)
 
         out_code = keep.tile([P, T], U32, name="out_code", align_bytes=64)
         out_scale = keep.tile([P, T], U8, name="out_scale", align_bytes=64)
         out_view = out_0.rearrange("(q t) v -> q t v", t=PACK)
         code_view = out_1[0].rearrange("q v t -> q (v t)").bitcast(I32)
+        dealt = [keep.tile([P, PACK, P], F32, name="dealt%d" % g) for g in range(GROUPS)]
 
-        for c, (v0, width) in enumerate(CHUNKS):
-            last = c == len(CHUNKS) - 1
-            groups = width // P
-            sums = [bank_tile((5, 6, 0, 3)[v0 // P + j], N) for j in range(groups)]
-            dealt = [keep.tile([P, PACK, P], F32, name="dealt%d_%d" % (c, j)) for j in range(groups)]
+        def drain(g, bank, b0, b1):
+            nc.scalar.activation(
+                dealt[g][:, :, QUAD * b0 : QUAD * b1],
+                bank[:, b0 * P : b1 * P].rearrange("v (q t) -> v t q", t=PACK),
+                ACT.Copy,
+                scale=inverse[:, g : g + 1],
+            )
 
-            def drain(j, bank, b0, b1):
-                nc.scalar.activation(
-                    dealt[j][:, :, 32 * b0 : 32 * b1],
-                    bank[:, b0 * P : b1 * P].rearrange("v (q t) -> v t q", t=PACK),
-                    ACT.Copy,
-                    scale=inverse[:, v0 // P + j : v0 // P + j + 1],
-                )
-
-            for b in range(BLOCKS):
+        for v0, width in CHUNKS:
+            last = v0 + width == T
+            groups = range(v0 // P, (v0 + width) // P)
+            targets = [sums[g] for g in groups]
+            for b in range(1, BLOCKS):
                 if last and b == BLOCKS - 1:
-                    drain(0, sums[0], 0, b)
-                    sums = [bank_tile(4, N)]
+                    drain(groups[0], targets[0], 0, b)
+                    targets = [work[2]]
                 for d in range(D):
-                    picked = ring.tile([P, width], F32, name="picked")
-                    nc.vector.tensor_tensor(
-                        picked[:],
-                        y[b][:].indirect(lists[d][:, v0 // 16 : (v0 + width) // 16]),
-                        weights[c][:, d, :],
-                        ALU.mult,
-                    )
-                    for j in range(groups):
-                        nc.tensor.matmul(
-                            sums[j][:, b * P : (b + 1) * P],
-                            picked[:, j * P : (j + 1) * P],
-                            ident[:],
-                            start=(d == 0),
-                            stop=(d == D - 1),
-                            is_transpose=True,
-                        )
-            result = keep.tile([P, PACK, width], F32, name="result%d" % c)
-            rounded = keep.tile([P, width, PACK], BF16, name="rounded%d" % c, align_bytes=64)
-            for j in range(groups):
-                drain(j, sums[j], BLOCKS - 1 if last else 0, BLOCKS)
-                back = bank_tile(1 + (v0 // P + j) % 2, N).rearrange("q (t v) -> q t v", t=PACK)
+                    gather(b, d, v0, width, ring.tile([P, width], F32, name="picked"), targets)
+            result = keep.tile([P, PACK, width], F32, name="result%d" % v0)
+            rounded = keep.tile([P, width, PACK], BF16, name="rounded%d" % v0, align_bytes=64)
+            for j, g in enumerate(groups):
+                drain(g, targets[j], BLOCKS - 1 if last else 0, BLOCKS)
+                back = work[g % 2][:].rearrange("q (t v) -> q t v", t=PACK)
                 for t in range(PACK):
-                    nc.tensor.transpose(back[:, t, :], dealt[j][:, t, :], ident[:])
+                    nc.tensor.transpose(back[:, t, :], dealt[g][:, t, :], ident[:])
                 if last:
-                    nc.vector.tensor_copy(rounded[:], back[:].rearrange("q t v -> q v t"))
+                    nc.vector.tensor_copy(rounded[:], back.rearrange("q t v -> q v t"))
                     for h in range(2):
                         rows = slice(2 * h, 2 * h + 2)
                         nc.scalar.copy(result[:, rows, :], back[:, rows, :])
-                        queue = nc.scalar if h else nc.sync
-                        queue.dma_start(out_view[:, rows, v0 : v0 + width], result[:, rows, :])
+                        nc.scalar.dma_start(out_view[:, rows, v0 : v0 + width], result[:, rows, :])
                 else:
-                    nc.scalar.copy(result[:, :, j * P : (j + 1) * P], back[:])
-                    nc.scalar.copy(rounded[:, j * P : (j + 1) * P, :], back[:].rearrange("q t v -> q v t"))
+                    nc.scalar.copy(result[:, :, j * P : (j + 1) * P], back)
+                    nc.scalar.copy(rounded[:, j * P : (j + 1) * P, :], back.rearrange("q t v -> q v t"))
             nc.vector.quantize_mx(
                 out=out_code[:, v0 : v0 + width].bitcast(FP8X4),
                 scales=out_scale[:, v0 : v0 + width],
@@ -207,6 +201,7 @@ def tile_picked_wgatv_none_lo_kernel(
             if not last:
                 nc.sync.dma_start(out_view[:, :, v0 : v0 + width], result[:])
             nc.sync.dma_start(code_view[:, v0 : v0 + width], out_code[:, v0 : v0 + width].bitcast(I32))
-        for q in range(4):
-            queue = nc.sync if q < 2 else nc.scalar
-            queue.dma_start(out_2[0, 4 * q : 4 * q + 4, :].bitcast(I32), out_scale[32 * q : 32 * q + 4, :].bitcast(I32))
+        for q in range(P // QUAD):
+            nc.sync.dma_start(
+                out_2[0, 4 * q : 4 * q + 4, :].bitcast(I32), out_scale[QUAD * q : QUAD * q + 4, :].bitcast(I32)
+            )

from contextlib import ExitStack

import concourse.mybir as mybir
from concourse.masks import make_identity

K, T, D, N = 512, 512, 4, 512
P = 128
PACK = 4
QUAD = 32
BLOCKS = N // P
GROUPS = T // P
SPARE = P - D * GROUPS
PAD = 8
FLOPS = 2 * K * N * T
BYTES = K * T + K * T // 32 + 4 * K * N + 4 * D * T + 2 * D * P * T // 16 + 4 * N * T + N * T + N * T // 32

F32 = mybir.dt.float32
BF16 = mybir.dt.bfloat16
U32 = mybir.dt.uint32
I32 = mybir.dt.int32
U16 = mybir.dt.uint16
U8 = mybir.dt.uint8
FP8X4 = mybir.dt.float8_e4m3fn_x4
ALU = mybir.AluOpType
ACT = mybir.ActivationFunctionType
AXIS_X = mybir.AxisListType.X

CHUNKS = ((0, 256), (256, 128), (384, 128))


def tile_picked_wgatv_none_lo_kernel(
    tc, x_words, x_scales, w1, score, pos1, pos2, pos3, pos4, out_0, out_1, out_2
):
    nc = tc.nc
    with ExitStack() as ctx:
        keep = ctx.enter_context(tc.tile_pool(name="keep", bufs=1))
        ring = ctx.enter_context(tc.tile_pool(name="ring", bufs=12))
        psum = ctx.enter_context(tc.psum_pool(name="psum", bufs=1))
        work = [psum.tile([P, T], F32, name="work%d" % i) for i in range(3)]
        sums = [psum.tile([P, N], F32, name="sums%d" % g) for g in range(GROUPS)]

        x_scale = keep.tile([P, T], U8, name="x_scale", align_bytes=64)
        nc.vector.memset(x_scale[:].bitcast(I32), 0)
        staged = keep.tile([P, P * PACK], BF16, name="staged", align_bytes=64)
        score_rows = staged[:].bitcast(F32)[:, 0:P]
        nc.vector.memset(score_rows[0:SPARE, :], 0.0)
        y = [keep.tile([P, T + PAD if b == 0 else T], F32, name="y%d" % b) for b in range(BLOCKS)]
        nc.vector.memset(y[0][:, T:], 0.0)
        ident = keep.tile([P, P], F32, name="ident")
        make_identity(nc, ident[:])

        score_view = score.rearrange("d r (g n) -> (d r g) n", n=P)
        nc.sync.dma_start(score_rows[SPARE:P, :], score_view[0 : D * P * GROUPS : P + 1, :])
        w_view = w1.rearrange("(p j) m -> p j m", j=PACK)
        w_first = keep.tile([P, PACK, P], F32, name="w_first")
        nc.sync.dma_start(w_first[:], w_view[:, :, 0:P])
        x_code = keep.tile([P, T], U32, name="x_code", align_bytes=64)
        nc.sync.dma_start(x_code[:].bitcast(I32), x_words[0].rearrange("p c r -> p (c r)").bitcast(I32))
        w_second = keep.tile([P, PACK, P], F32, name="w_second")
        nc.sync.dma_start(w_second[:], w_view[:, :, P : 2 * P])
        for q in range(P // QUAD):
            nc.sync.dma_start(
                x_scale[QUAD * q : QUAD * q + 4, :].bitcast(I32), x_scales[0, 4 * q : 4 * q + 4, :].bitcast(I32)
            )
        lists = [keep.tile([P, T // 16], U16, name="offsets%d" % d) for d in range(D)]
        nc.sync.dma_start(lists[0][:], pos1)
        w_rest = keep.tile([P, PACK, 2 * P], F32, name="w_rest")
        nc.sync.dma_start(w_rest[:], w_view[:, :, 2 * P : 4 * P])
        for offsets, pos in zip(lists[1:], (pos2, pos3, pos4)):
            nc.sync.dma_start(offsets[:], pos)
        w_raw = [w_first[:], w_second[:], w_rest[:, :, 0:P], w_rest[:, :, P : 2 * P]]

        first = keep.tile([P, T], F32, name="first", align_bytes=64)

        def project(b, banks):
            if b < 2:
                grouped = staged[:]
                nc.vector.tensor_copy(
                    grouped.rearrange("p (m j) -> p m j", j=PACK), w_raw[b].rearrange("p j m -> p m j")
                )
            else:
                grouped = first[:, T // 2 :].bitcast(BF16)
                nc.scalar.copy(grouped.rearrange("p (m j) -> p m j", j=PACK), w_raw[b].rearrange("p j m -> p m j"))
            w_code = keep.tile([P, P], U32, name="w_code%d" % b, align_bytes=64)
            w_scale = keep.tile([P, P], U8, name="w_scale%d" % b, align_bytes=64)
            nc.vector.quantize_mx(out=w_code[:].bitcast(FP8X4), scales=w_scale[:], in_=grouped)
            width = T // len(banks)
            for h, bank in enumerate(banks):
                cols = slice(h * width, (h + 1) * width)
                nc.tensor.matmul_mx(
                    out=bank[:, 0:width],
                    lhsT=w_code[:].bitcast(FP8X4),
                    lhsT_scale=w_scale[:],
                    rhs=x_code[:, cols].bitcast(FP8X4),
                    rhs_scale=x_scale[:, cols],
                    start=True,
                    stop=True,
                )
                if h == len(banks) - 1:
                    nc.scalar.copy(y[b][:, cols], bank[:, 0:width])
                else:
                    nc.vector.tensor_copy(y[b][:, cols], bank[:, 0:width])

        nc.tensor.transpose(work[0][:, 0:P], score_rows, ident[:])
        scores = work[0][:, SPARE:P].rearrange("p (d g) -> p d g", d=D)
        top = keep.tile([P, GROUPS], F32, name="top")
        nc.vector.tensor_reduce(top[:], scores.rearrange("p d g -> p g d"), AXIS_X, ALU.max)
        shifted = keep.tile([P, D, GROUPS], F32, name="shifted")
        nc.vector.tensor_tensor(shifted[:], scores, top[:].unsqueeze(1).to_broadcast([P, D, GROUPS]), ALU.subtract)

        weights = [keep.tile([P, T], F32, name="weights%d" % d) for d in range(D)]

        def spread(d, bank):
            for g in range(GROUPS):
                nc.tensor.transpose(
                    bank[:, g * P : (g + 1) * P], shifted[:, d, g : g + 1].to_broadcast([P, P]), ident[:]
                )
            nc.scalar.activation(weights[d][:], bank[:], ACT.Exp)

        def gather(b, d, v0, width, picked, targets):
            nc.vector.tensor_tensor(
                picked[:],
                y[b][:].indirect(lists[d][:, v0 // 16 : (v0 + width) // 16]),
                weights[d][:, v0 : v0 + width],
                ALU.mult,
            )
            for j, bank in enumerate(targets):
                nc.tensor.matmul(
                    bank[:, b * P : (b + 1) * P],
                    picked[:, j * P : (j + 1) * P],
                    ident[:],
                    start=(d == 0),
                    stop=(d == D - 1),
                    is_transpose=True,
                )

        spread(0, work[1])
        project(0, [work[0], work[2]])
        spread(1, work[0])
        spread(2, work[2])
        project(1, [work[1]])
        spread(3, work[0])

        gather(0, 0, 0, T, first, sums)
        project(2, [work[1]])
        project(3, [work[2]])
        exps = first[:, 0 : D * GROUPS].rearrange("p (d g) -> p d g", d=D)
        nc.scalar.activation(exps, shifted[:], ACT.Exp)
        total = keep.tile([P, GROUPS], F32, name="total")
        nc.vector.tensor_reduce(total[:], exps.rearrange("p d g -> p g d"), AXIS_X, ALU.add)
        inverse = keep.tile([P, GROUPS], F32, name="inverse")
        nc.vector.reciprocal(inverse[:], total[:])
        for d in range(1, D):
            gather(0, d, 0, T, ring.tile([P, T], F32, name="picked"), sums)

        out_code = keep.tile([P, T], U32, name="out_code", align_bytes=64)
        out_scale = keep.tile([P, T], U8, name="out_scale", align_bytes=64)
        out_view = out_0.rearrange("(q t) v -> q t v", t=PACK)
        code_view = out_1[0].rearrange("q v t -> q (v t)").bitcast(I32)
        dealt = [keep.tile([P, PACK, P], F32, name="dealt%d" % g) for g in range(GROUPS)]

        def drain(g, bank, b0, b1):
            nc.scalar.activation(
                dealt[g][:, :, QUAD * b0 : QUAD * b1],
                bank[:, b0 * P : b1 * P].rearrange("v (q t) -> v t q", t=PACK),
                ACT.Copy,
                scale=inverse[:, g : g + 1],
            )

        for v0, width in CHUNKS:
            last = v0 + width == T
            groups = range(v0 // P, (v0 + width) // P)
            targets = [sums[g] for g in groups]
            for b in range(1, BLOCKS):
                if last and b == BLOCKS - 1:
                    drain(groups[0], targets[0], 0, b)
                    targets = [work[2]]
                for d in range(D):
                    gather(b, d, v0, width, ring.tile([P, width], F32, name="picked"), targets)
            result = keep.tile([P, PACK, width], F32, name="result%d" % v0)
            rounded = keep.tile([P, width, PACK], BF16, name="rounded%d" % v0, align_bytes=64)
            for j, g in enumerate(groups):
                drain(g, targets[j], BLOCKS - 1 if last else 0, BLOCKS)
                back = work[g % 2][:].rearrange("q (t v) -> q t v", t=PACK)
                for t in range(PACK):
                    nc.tensor.transpose(back[:, t, :], dealt[g][:, t, :], ident[:])
                if last:
                    nc.vector.tensor_copy(rounded[:], back.rearrange("q t v -> q v t"))
                    for h in range(2):
                        rows = slice(2 * h, 2 * h + 2)
                        nc.scalar.copy(result[:, rows, :], back[:, rows, :])
                        nc.scalar.dma_start(out_view[:, rows, v0 : v0 + width], result[:, rows, :])
                else:
                    nc.scalar.copy(result[:, :, j * P : (j + 1) * P], back)
                    nc.scalar.copy(rounded[:, j * P : (j + 1) * P, :], back.rearrange("q t v -> q v t"))
            nc.vector.quantize_mx(
                out=out_code[:, v0 : v0 + width].bitcast(FP8X4),
                scales=out_scale[:, v0 : v0 + width],
                in_=rounded[:].rearrange("q v t -> q (v t)"),
            )
            if not last:
                nc.sync.dma_start(out_view[:, :, v0 : v0 + width], result[:])
            nc.sync.dma_start(code_view[:, v0 : v0 + width], out_code[:, v0 : v0 + width].bitcast(I32))
        for q in range(P // QUAD):
            nc.sync.dma_start(
                out_2[0, 4 * q : 4 * q + 4, :].bitcast(I32), out_scale[QUAD * q : QUAD * q + 4, :].bitcast(I32)
            )
